import numpy as np
import ml_dtypes


def mxq(x, axis, fmt="e4m3"):
    dtype, down = {"e4m3": (ml_dtypes.float8_e4m3fn, 7), "e5m2": (ml_dtypes.float8_e5m2, 14)}[fmt]
    v = np.moveaxis(np.asarray(x, np.float32).astype(ml_dtypes.bfloat16).astype(np.float64), axis, -1)
    blocks = v.reshape(v.shape[:-1] + (-1, 32))
    amax = np.abs(blocks).max(-1, keepdims=True)
    byte = np.maximum(np.where(amax > 0, np.frexp(amax)[1] - 1 + 127, 0) - down, 1)
    scale = np.exp2(byte - 127.0)
    codes = (blocks / scale).astype(np.float32).astype(dtype).astype(np.float64)
    return np.moveaxis((codes * scale).reshape(v.shape), -1, axis)


WIDE = False


def mx_kscale(k):
    if not WIDE:
        return np.ones(k)
    levels = np.array([10, -10, 5, -5, 0])
    if k % 512:
        return np.exp2(np.random.permutation(np.resize(levels, k // 32))).repeat(32)
    a = np.empty((k // 512, 16))
    for p in range(k // 512):
        a[p, :8] = np.random.permutation(np.resize(levels, 8))
        for g in range(8):
            far = levels[np.abs(levels - a[p, g]) >= 10]
            a[p, g + 8] = far[np.random.randint(len(far))]
    return np.exp2(a.ravel()).repeat(32)


def f64(x):
    return np.asarray(x).astype(np.float64)


def striped(idx):
    return np.tile(idx.reshape(-1, 16).T, (8, 1)).astype(np.uint16)


def unstriped(offs):
    return offs[:16].T.reshape(-1).astype(np.int64)


def pack_weight(w):
    k, n = w.shape
    w = f64(np.asarray(w, np.float32).astype(ml_dtypes.bfloat16)).reshape(k // 32, 32, n)
    amax = np.abs(w).max(1)
    byte = np.clip(np.where(amax > 0, np.frexp(amax)[1] - 1 + 127 - 7, 1), 1, 254)
    scaled = (w * np.exp2(127.0 - byte)[:, None, :]).reshape(k, n).astype(np.float32)
    words = np.ascontiguousarray(scaled.reshape(k // 512, 128, 4, n).transpose(0, 1, 3, 2)).astype(ml_dtypes.float8_e4m3fn).view(np.uint8)
    return words, np.ascontiguousarray(byte.astype(np.uint8).reshape(k // 512, 16, n))


def unpack_weight(words, scales):
    g, p, n, _ = words.shape
    vals = np.ascontiguousarray(words).view(ml_dtypes.float8_e4m3fn).astype(np.float64) * np.repeat(np.exp2(scales.astype(np.float64) - 127.0), 8, axis=1)[..., None]
    return vals.transpose(0, 1, 3, 2).reshape(g * 512, n)


K, T, S, V, R = 1024, 2048, 512, 512, 512
P = 2 ** 7


def setup_inputs():
    n = np.random.standard_normal
    s = mx_kscale(K)[:, None]
    packed_xT = pack_weight(n((K, T)) * s)
    return {
        "x_words": packed_xT[0],
        "x_scales": packed_xT[1],
        "hT": (n((K, V)) / np.sqrt(K) / s).astype(np.float32),
        "alpha": (n((V, R))).astype(np.float32),
        "m1": (np.tile((np.random.uniform(size=R) < 0.8) * 1.0, (P, 1))).astype(np.float32),
        "m2": (np.tile((np.random.uniform(size=R) < 0.4) * 1.0, (P, 1))).astype(np.float32),
        "offs": striped(np.random.permutation(T)[:S]),
        "lab": striped(np.random.randint(0, S, R)),
    }


def reference(x_words, x_scales, hT, alpha, m1, m2, offs, lab):
    hTq = mxq(f64(hT), 0, "e4m3")
    xq = unpack_weight(x_words, x_scales)[:, unstriped(offs)]
    y = hTq.T @ xq
    ee = np.exp(y)
    s0 = np.log(ee.sum(axis=1, keepdims=True))
    lp = y - s0
    gg = lp[:, unstriped(lab)]
    ea = np.exp(f64(alpha))
    return np.exp(0.5 * (gg + np.log(ea + (np.pad(ea, ((0, 0), (1, 0)))[:, :S]) * f64(m1)[:1] + (np.pad(ea, ((0, 0), (2, 0)))[:, :S]) * f64(m2)[:1]) + 4.0))

@@ -1,0 +1,183 @@
+import math
+from contextlib import ExitStack
+
+import concourse.mybir as mybir
+from concourse.masks import make_identity
+
+F32 = mybir.dt.float32
+BF16 = mybir.dt.bfloat16
+I32 = mybir.dt.int32
+U32 = mybir.dt.uint32
+U16 = mybir.dt.uint16
+U8 = mybir.dt.uint8
+FP8X4 = mybir.dt.float8_e4m3fn_x4
+ALU = mybir.AluOpType
+ACT = mybir.ActivationFunctionType
+AX = mybir.AxisListType
+
+P = 128
+K, T, S, V, R = 1024, 2048, 512, 512, 512
+PASSES = K // 512
+TILES = V // P
+BLOCKS = R // P
+PAD = 4
+FLOPS = 2 * K * V * S
+
+
+def tile_picked_yctc_root_p_kernel(tc, x_words, x_scales, hT, alpha, m1, m2, offs, lab, out):
+    nc = tc.nc
+    with ExitStack() as ctx:
+        keep = ctx.enter_context(tc.tile_pool(name="keep", bufs=1))
+        psum = ctx.enter_context(tc.psum_pool(name="psum", bufs=1))
+
+        offs_t = keep.tile([P, S // 16], U16, name="offs_t")
+        lab_t = keep.tile([P, R // 16], U16, name="lab_t")
+        ident = keep.tile([P, P], F32, name="ident")
+        neg_half = keep.tile([P, 1], F32, name="neg_half")
+        win = [keep.tile([P, 4 * S], F32, name=f"win{i}") for i in range(TILES)]
+        ea = [keep.tile([P, PAD + R], F32, name=f"ea{i}") for i in range(TILES)]
+        rootT = [win[TILES - 1 - i][:, S : 2 * S] for i in range(TILES)]
+        euler = keep.tile([P, TILES], F32, name="euler")
+        picked = [keep.tile([P, R], F32, name=f"picked{i}") for i in range(TILES)]
+        res = [keep.tile([P, R], F32, name=f"res{i}") for i in range(TILES)]
+        mcol = [keep.tile([P, BLOCKS], F32, name=f"mcol{n}") for n in range(2)]
+        scale_t = keep.tile([P, TILES], F32, name="scale_t")
+        xw = [keep.tile([P, T], I32, name=f"xw{o}") for o in range(PASSES)]
+        xs = keep.tile([P, T], U8, name="xs")
+        hraw = [[keep.tile([P, 4, V // 2], F32, name=f"hraw{o}_{u}", tag=f"stage{o}_{u}", align_bytes=64) for u in range(2)] for o in range(PASSES)]
+        al = [keep.tile([P, R], F32, name=f"al{i}", tag=f"slot{i}", align_bytes=64) for i in range(TILES)]
+        hb = {}
+        hq = [[keep.tile([P, V // 2], U32, name=f"hq{o}_{u}", align_bytes=64) for u in range(2)] for o in range(PASSES)]
+        hs = [[keep.tile([P, V // 2], U8, name=f"hs{o}_{u}", align_bytes=64) for u in range(2)] for o in range(PASSES)]
+        neg_amax = keep.tile([P, TILES], F32, name="neg_amax")
+        lift = keep.tile([P, TILES], F32, name="lift")
+        neg_ymax = keep.tile([P, TILES], F32, name="neg_ymax")
+        shift = keep.tile([P, TILES], F32, name="shift")
+        total = keep.tile([P, TILES], F32, name="total")
+        rinv = keep.tile([P, TILES], F32, name="rinv")
+
+        nc.gpsimd.memset(xs[:].bitcast(I32), 0)
+        for i in range(TILES):
+            nc.vector.memset(ea[i][:, 0:PAD], 0.0)
+        nc.gpsimd.memset(neg_half[:], -0.5)
+        make_identity(nc, ident[:])
+
+        for i in range(TILES):
+            nc.sync.dma_start(al[i][:], alpha[i * P : (i + 1) * P, :])
+        for n, m in enumerate((m1, m2)):
+            nc.scalar.dma_start(mcol[n][:], m[0].rearrange("(p b) -> p b", b=BLOCKS))
+
+        def load_h(o, u):
+            nc.sync.dma_start(hraw[o][u][:], hT[512 * o : 512 * (o + 1), u * 256 : (u + 1) * 256].rearrange("(p j) v -> p j v", j=4))
+
+        early = [(0, 0), (1, 0), (0, 1)]
+        for o, u in early:
+            load_h(o, u)
+        for q in range(4):
+            nc.sync.dma_start(xs[32 * q : 32 * q + 8, :].bitcast(I32), x_scales.bitcast(I32)[:, 4 * q : 4 * q + 4, :])
+        nc.sync.dma_start(offs_t[:], offs)
+        for o in range(PASSES):
+            nc.sync.dma_start(xw[o][:], x_words[o].rearrange("p n t -> p (n t)").bitcast(I32))
+        load_h(1, 1)
+        nc.sync.dma_start(lab_t[:], lab)
+
+        for i in range(TILES):
+            nc.vector.tensor_reduce(neg_amax[:, i : i + 1], al[i][:], AX.X, ALU.max, negate=True)
+            nc.scalar.activation(ea[i][:, PAD : PAD + R], al[i][:], ACT.Exp, bias=neg_amax[:, i : i + 1], scale=1.0)
+        nc.gpsimd.tensor_scalar(shift[:], neg_amax[:], -0.5, 2.0, ALU.mult, ALU.add)
+        nc.gpsimd.tensor_scalar(euler[:], neg_amax[:], 0.0, math.e, ALU.mult, ALU.add)
+        nc.gpsimd.tensor_tensor(lift[:], euler[:], shift[:], ALU.pow)
+
+        mask = [psum.tile([P, R], F32, name=f"mask{n}", tag=f"root{2 + n}") for n in range(2)]
+        for n in range(2):
+            for b in range(BLOCKS):
+                nc.tensor.transpose(mask[n][:, b * P : (b + 1) * P], mcol[n][:, b : b + 1].to_broadcast([P, P]), ident[:])
+        root = []
+
+        def interleave(engine_copy, o, u):
+            hb[o, u] = keep.tile([P, V // 2, 4], BF16, name=f"hb{o}_{u}", tag=f"slot{TILES - 1 - 2 * u - o}", align_bytes=64)
+            engine_copy(
+                hb[o, u][:].rearrange("p (c i) j -> p c j i", i=4),
+                hraw[o][u][:].rearrange("p j (c i) -> p c j i", i=4),
+            )
+
+        def quantise(o, u):
+            nc.vector.quantize_mx(out=hq[o][u][:].bitcast(FP8X4), scales=hs[o][u][:], in_=hb[o, u][:].rearrange("p c j -> p (c j)"))
+
+        for o, u in early:
+            interleave(nc.scalar.copy, o, u)
+
+        for i in range(TILES):
+            for n in range(2):
+                nc.vector.tensor_tensor(
+                    win[i][:, (2 + n) * S : (3 + n) * S].rearrange("p (c b) -> p c b", b=BLOCKS),
+                    ea[i][:, PAD - 1 - n : PAD - 1 - n + R].rearrange("p (c b) -> p c b", b=BLOCKS),
+                    mask[n][:].rearrange("p (b c) -> p c b", b=BLOCKS),
+                    ALU.mult,
+                )
+        for i in range(TILES):
+            sumT = psum.tile([P, R], F32, name="sumT", tag=f"work{i}")
+            for b in range(BLOCKS):
+                terms = [
+                    ea[i][:, PAD + b * P : PAD + (b + 1) * P],
+                    win[i][:, 2 * S + b * P : 2 * S + (b + 1) * P],
+                    win[i][:, 3 * S + b * P : 3 * S + (b + 1) * P],
+                ]
+                for n, term in enumerate(terms):
+                    nc.tensor.matmul(sumT[:, b * P : (b + 1) * P], term, ident[:], start=(n == 0), stop=(n == 2), is_transpose=True)
+            nc.scalar.activation(rootT[i], sumT[:], ACT.Sqrt)
+
+        for i in range(TILES):
+            root.append(psum.tile([P, R], F32, name=f"root{i}", tag=f"root{i}"))
+            for b in range(BLOCKS):
+                nc.tensor.transpose(root[i][:, b * P : (b + 1) * P], rootT[i][:, b * P : (b + 1) * P], ident[:])
+
+        for o, u in early:
+            quantise(o, u)
+        xg = [keep.tile([P, S], U32, name=f"xg{o}", tag=f"stage{o}_0", align_bytes=64) for o in range(PASSES)]
+        sg = keep.tile([P, S], U8, name="sg", tag="stage0_1", align_bytes=64)
+        nc.vector.tensor_copy(sg[:], xs[:].indirect(offs_t[:]))
+        nc.vector.tensor_copy(xg[0][:], xw[0][:].bitcast(U32).indirect(offs_t[:]))
+        nc.vector.tensor_copy(xg[1][:], xw[1][:].bitcast(U32).indirect(offs_t[:]))
+
+        y = [psum.tile([P, S], F32, name=f"y{i}", tag=f"work{TILES - 1 - i}") for i in range(TILES)]
+
+        def product(i, o):
+            u, w = divmod(i, 2)
+            cols = slice(w * P, (w + 1) * P)
+            nc.tensor.matmul_mx(
+                out=y[i][:],
+                lhsT=hq[o][u][:, cols].bitcast(FP8X4),
+                lhsT_scale=hs[o][u][:, cols],
+                rhs=xg[o][:].bitcast(FP8X4),
+                rhs_scale=sg[4 * o : P, :],
+                start=(o == 0),
+                stop=(o == PASSES - 1),
+            )
+
+        def row_max_and_sum(i):
+            one = slice(i, i + 1)
+            nc.vector.tensor_reduce(neg_ymax[:, one], y[i][:], AX.X, ALU.max, negate=True)
+            nc.scalar.activation(rootT[TILES - 1 - i], y[i][:], ACT.Exp, bias=neg_ymax[:, one], accum_out=total[:, one])
+            nc.gpsimd.tensor_tensor(rinv[:, one], total[:, one], neg_half[:], ALU.pow)
+            nc.gpsimd.tensor_tensor(scale_t[:, one], rinv[:, one], lift[:, one], ALU.mult)
+
+        def look_up(i):
+            nc.vector.tensor_scalar(win[i][:, 0:S], y[i][:], neg_ymax[:, i : i + 1], None, ALU.add)
+            nc.scalar.activation(picked[i][:], win[i][:].indirect(lab_t[:]), ACT.Exp, scale=0.5)
+
+        interleave(nc.vector.tensor_copy, 1, 1)
+        quantise(1, 1)
+        for pair in range(2):
+            for o in range(PASSES):
+                for i in range(2 * pair, 2 * pair + 2):
+                    product(i, o)
+        row_max_and_sum(0)
+        for i in range(TILES):
+            if i + 1 < TILES:
+                row_max_and_sum(i + 1)
+            look_up(i)
+        for i in range(TILES):
+            one = slice(i, i + 1)
+            nc.vector.scalar_tensor_tensor(res[i][:], picked[i][:], scale_t[:, one], root[i][:], ALU.mult, ALU.mult)
+            nc.sync.dma_start(out[i * P : (i + 1) * P, :], res[i][:])

@@ -33,33 +33,32 @@ def tile_picked_yctc_root_p_kernel(tc, x_words, x_scales, hT, alpha, m1, m2, off
         offs_t = keep.tile([P, S // 16], U16, name="offs_t")
         lab_t = keep.tile([P, R // 16], U16, name="lab_t")
         ident = keep.tile([P, P], F32, name="ident")
-        neg_half = keep.tile([P, 1], F32, name="neg_half")
+        neg_half = keep.tile([P, PAD], F32, name="neg_half")
         win = [keep.tile([P, 4 * S], F32, name=f"win{i}") for i in range(TILES)]
-        ea = [keep.tile([P, PAD + R], F32, name=f"ea{i}") for i in range(TILES)]
+        ea = [keep.tile([P, PAD + R], F32, name=f"ea{i}", tag=f"exp{i}", align_bytes=64) for i in range(TILES)]
         rootT = [win[TILES - 1 - i][:, S : 2 * S] for i in range(TILES)]
         euler = keep.tile([P, TILES], F32, name="euler")
         picked = [keep.tile([P, R], F32, name=f"picked{i}") for i in range(TILES)]
         res = [keep.tile([P, R], F32, name=f"res{i}") for i in range(TILES)]
         mcol = [keep.tile([P, BLOCKS], F32, name=f"mcol{n}") for n in range(2)]
         scale_t = keep.tile([P, TILES], F32, name="scale_t")
-        xw = [keep.tile([P, T], I32, name=f"xw{o}") for o in range(PASSES)]
-        xs = keep.tile([P, T], U8, name="xs")
-        hraw = [[keep.tile([P, 4, V // 2], F32, name=f"hraw{o}_{u}", tag=f"stage{o}_{u}", align_bytes=64) for u in range(2)] for o in range(PASSES)]
+        xw = [keep.tile([P, T], I32, name=f"xw{o}", tag=f"words{o}", align_bytes=64) for o in range(PASSES)]
+        xs = keep.tile([P, T], U8, name="xs", tag="planes", align_bytes=64)
+        hraw = [[keep.tile([P, 4, V // 2], F32, name=f"hraw{o}_{u}") for u in range(2)] for o in range(PASSES)]
         al = [keep.tile([P, R], F32, name=f"al{i}", tag=f"slot{i}", align_bytes=64) for i in range(TILES)]
         hb = {}
-        hq = [[keep.tile([P, V // 2], U32, name=f"hq{o}_{u}", align_bytes=64) for u in range(2)] for o in range(PASSES)]
+        hq = {}
         hs = [[keep.tile([P, V // 2], U8, name=f"hs{o}_{u}", align_bytes=64) for u in range(2)] for o in range(PASSES)]
         neg_amax = keep.tile([P, TILES], F32, name="neg_amax")
         lift = keep.tile([P, TILES], F32, name="lift")
-        neg_ymax = keep.tile([P, TILES], F32, name="neg_ymax")
         shift = keep.tile([P, TILES], F32, name="shift")
         total = keep.tile([P, TILES], F32, name="total")
         rinv = keep.tile([P, TILES], F32, name="rinv")
 
+        nc.vector.memset(neg_half[:], -0.5)
         nc.gpsimd.memset(xs[:].bitcast(I32), 0)
         for i in range(TILES):
-            nc.vector.memset(ea[i][:, 0:PAD], 0.0)
-        nc.gpsimd.memset(neg_half[:], -0.5)
+            nc.scalar.activation(ea[i][:, 0:PAD], neg_half[:], ACT.Exp, scale=4096.0)
         make_identity(nc, ident[:])
 
         for i in range(TILES):
@@ -85,7 +84,7 @@ def tile_picked_yctc_root_p_kernel(tc, x_words, x_scales, hT, alpha, m1, m2, off
             nc.vector.tensor_reduce(neg_amax[:, i : i + 1], al[i][:], AX.X, ALU.max, negate=True)
             nc.scalar.activation(ea[i][:, PAD : PAD + R], al[i][:], ACT.Exp, bias=neg_amax[:, i : i + 1], scale=1.0)
         nc.gpsimd.tensor_scalar(shift[:], neg_amax[:], -0.5, 2.0, ALU.mult, ALU.add)
-        nc.gpsimd.tensor_scalar(euler[:], neg_amax[:], 0.0, math.e, ALU.mult, ALU.add)
+        nc.gpsimd.tensor_scalar(euler[:], neg_half[:], 0.0, math.e, ALU.mult, ALU.add)
         nc.gpsimd.tensor_tensor(lift[:], euler[:], shift[:], ALU.pow)
 
         mask = [psum.tile([P, R], F32, name=f"mask{n}", tag=f"root{2 + n}") for n in range(2)]
@@ -102,31 +101,35 @@ def tile_picked_yctc_root_p_kernel(tc, x_words, x_scales, hT, alpha, m1, m2, off
             )
 
         def quantise(o, u):
-            nc.vector.quantize_mx(out=hq[o][u][:].bitcast(FP8X4), scales=hs[o][u][:], in_=hb[o, u][:].rearrange("p c j -> p (c j)"))
+            hq[o, u] = keep.tile([P, V // 2], U32, name=f"hq{o}_{u}", tag=f"exp{(1 + o + 2 * u) % TILES}", align_bytes=64)
+            nc.vector.quantize_mx(out=hq[o, u][:].bitcast(FP8X4), scales=hs[o][u][:], in_=hb[o, u][:].rearrange("p c j -> p (c j)"))
 
         for o, u in early:
             interleave(nc.scalar.copy, o, u)
 
+        sumT = [psum.tile([P, R], F32, name=f"sumT{i}", tag=f"work{i}") for i in range(TILES)]
+
+        def add_turned(i, term, first, last):
+            for b in range(BLOCKS):
+                cols = slice(b * P, (b + 1) * P)
+                nc.tensor.matmul(
+                    sumT[i][:, cols], term[:, cols], ident[:],
+                    start=(first and b == 0), stop=(last and b == BLOCKS - 1), is_transpose=True,
+                )
+
+        for i in range(TILES):
+            add_turned(i, ea[i][:, PAD : PAD + R], True, False)
         for i in range(TILES):
             for n in range(2):
+                term = win[i][:, (2 + n) * S : (3 + n) * S]
                 nc.vector.tensor_tensor(
-                    win[i][:, (2 + n) * S : (3 + n) * S].rearrange("p (c b) -> p c b", b=BLOCKS),
+                    term.rearrange("p (c b) -> p c b", b=BLOCKS),
                     ea[i][:, PAD - 1 - n : PAD - 1 - n + R].rearrange("p (c b) -> p c b", b=BLOCKS),
                     mask[n][:].rearrange("p (b c) -> p c b", b=BLOCKS),
                     ALU.mult,
                 )
-        for i in range(TILES):
-            sumT = psum.tile([P, R], F32, name="sumT", tag=f"work{i}")
-            for b in range(BLOCKS):
-                terms = [
-                    ea[i][:, PAD + b * P : PAD + (b + 1) * P],
-                    win[i][:, 2 * S + b * P : 2 * S + (b + 1) * P],
-                    win[i][:, 3 * S + b * P : 3 * S + (b + 1) * P],
-                ]
-                for n, term in enumerate(terms):
-                    nc.tensor.matmul(sumT[:, b * P : (b + 1) * P], term, ident[:], start=(n == 0), stop=(n == 2), is_transpose=True)
-            nc.scalar.activation(rootT[i], sumT[:], ACT.Sqrt)
-
+                add_turned(i, term, False, n == 1)
+            nc.scalar.activation(rootT[i], sumT[i][:], ACT.Sqrt)
         for i in range(TILES):
             root.append(psum.tile([P, R], F32, name=f"root{i}", tag=f"root{i}"))
             for b in range(BLOCKS):
@@ -134,8 +137,8 @@ def tile_picked_yctc_root_p_kernel(tc, x_words, x_scales, hT, alpha, m1, m2, off
 
         for o, u in early:
             quantise(o, u)
-        xg = [keep.tile([P, S], U32, name=f"xg{o}", tag=f"stage{o}_0", align_bytes=64) for o in range(PASSES)]
-        sg = keep.tile([P, S], U8, name="sg", tag="stage0_1", align_bytes=64)
+        xg = [keep.tile([P, S], U32, name=f"xg{o}", tag=("planes", "words0")[o], align_bytes=64) for o in range(PASSES)]
+        sg = keep.tile([P, S], U8, name="sg", tag="slot1", align_bytes=64)
         nc.vector.tensor_copy(sg[:], xs[:].indirect(offs_t[:]))
         nc.vector.tensor_copy(xg[0][:], xw[0][:].bitcast(U32).indirect(offs_t[:]))
         nc.vector.tensor_copy(xg[1][:], xw[1][:].bitcast(U32).indirect(offs_t[:]))
@@ -147,7 +150,7 @@ def tile_picked_yctc_root_p_kernel(tc, x_words, x_scales, hT, alpha, m1, m2, off
             cols = slice(w * P, (w + 1) * P)
             nc.tensor.matmul_mx(
                 out=y[i][:],
-                lhsT=hq[o][u][:, cols].bitcast(FP8X4),
+                lhsT=hq[o, u][:, cols].bitcast(FP8X4),
                 lhsT_scale=hs[o][u][:, cols],
                 rhs=xg[o][:].bitcast(FP8X4),
                 rhs_scale=sg[4 * o : P, :],
@@ -159,7 +162,7 @@ def tile_picked_yctc_root_p_kernel(tc, x_words, x_scales, hT, alpha, m1, m2, off
             one = slice(i, i + 1)
             nc.vector.tensor_reduce(neg_ymax[:, one], y[i][:], AX.X, ALU.max, negate=True)
             nc.scalar.activation(rootT[TILES - 1 - i], y[i][:], ACT.Exp, bias=neg_ymax[:, one], accum_out=total[:, one])
-            nc.gpsimd.tensor_tensor(rinv[:, one], total[:, one], neg_half[:], ALU.pow)
+            nc.gpsimd.tensor_tensor(rinv[:, one], total[:, one], neg_half[:, 0:1], ALU.pow)
             nc.gpsimd.tensor_tensor(scale_t[:, one], rinv[:, one], lift[:, one], ALU.mult)
 
         def look_up(i):
@@ -168,6 +171,7 @@ def tile_picked_yctc_root_p_kernel(tc, x_words, x_scales, hT, alpha, m1, m2, off
 
         interleave(nc.vector.tensor_copy, 1, 1)
         quantise(1, 1)
+        neg_ymax = keep.tile([P, TILES], F32, name="neg_ymax", tag="slot0", align_bytes=64)
         for pair in range(2):
             for o in range(PASSES):
                 for i in range(2 * pair, 2 * pair + 2):
@@ -179,5 +183,9 @@ def tile_picked_yctc_root_p_kernel(tc, x_words, x_scales, hT, alpha, m1, m2, off
             look_up(i)
         for i in range(TILES):
             one = slice(i, i + 1)
-            nc.vector.scalar_tensor_tensor(res[i][:], picked[i][:], scale_t[:, one], root[i][:], ALU.mult, ALU.mult)
-            nc.sync.dma_start(out[i * P : (i + 1) * P, :], res[i][:])
+            pieces = 2 if i == TILES - 1 else 1
+            for h in range(pieces):
+                cols = slice(h * R // pieces, (h + 1) * R // pieces)
+                nc.vector.scalar_tensor_tensor(res[i][:, cols], picked[i][:, cols], scale_t[:, one], root[i][:, cols], ALU.mult, ALU.mult)
+                queue = nc.scalar if h == 1 else nc.sync
+                queue.dma_start(out[i * P : (i + 1) * P, cols], res[i][:, cols])

import math
from contextlib import ExitStack

import concourse.mybir as mybir
from concourse.masks import make_identity

F32 = mybir.dt.float32
BF16 = mybir.dt.bfloat16
I32 = mybir.dt.int32
U32 = mybir.dt.uint32
U16 = mybir.dt.uint16
U8 = mybir.dt.uint8
FP8X4 = mybir.dt.float8_e4m3fn_x4
ALU = mybir.AluOpType
ACT = mybir.ActivationFunctionType
AX = mybir.AxisListType

P = 128
K, T, S, V, R = 1024, 2048, 512, 512, 512
PASSES = K // 512
TILES = V // P
BLOCKS = R // P
PAD = 4
FLOPS = 2 * K * V * S


def tile_picked_yctc_root_p_kernel(tc, x_words, x_scales, hT, alpha, m1, m2, offs, lab, out):
    nc = tc.nc
    with ExitStack() as ctx:
        keep = ctx.enter_context(tc.tile_pool(name="keep", bufs=1))
        psum = ctx.enter_context(tc.psum_pool(name="psum", bufs=1))

        offs_t = keep.tile([P, S // 16], U16, name="offs_t")
        lab_t = keep.tile([P, R // 16], U16, name="lab_t")
        ident = keep.tile([P, P], F32, name="ident")
        neg_half = keep.tile([P, PAD], F32, name="neg_half")
        win = [keep.tile([P, 4 * S], F32, name=f"win{i}") for i in range(TILES)]
        ea = [keep.tile([P, PAD + R], F32, name=f"ea{i}", tag=f"exp{i}", align_bytes=64) for i in range(TILES)]
        rootT = [win[TILES - 1 - i][:, S : 2 * S] for i in range(TILES)]
        euler = keep.tile([P, TILES], F32, name="euler")
        picked = [keep.tile([P, R], F32, name=f"picked{i}") for i in range(TILES)]
        res = [keep.tile([P, R], F32, name=f"res{i}") for i in range(TILES)]
        mcol = [keep.tile([P, BLOCKS], F32, name=f"mcol{n}") for n in range(2)]
        scale_t = keep.tile([P, TILES], F32, name="scale_t")
        xw = [keep.tile([P, T], I32, name=f"xw{o}", tag=f"words{o}", align_bytes=64) for o in range(PASSES)]
        xs = keep.tile([P, T], U8, name="xs", tag="planes", align_bytes=64)
        hraw = [[keep.tile([P, 4, V // 2], F32, name=f"hraw{o}_{u}") for u in range(2)] for o in range(PASSES)]
        al = [keep.tile([P, R], F32, name=f"al{i}", tag=f"slot{i}", align_bytes=64) for i in range(TILES)]
        hb = {}
        hq = {}
        hs = [[keep.tile([P, V // 2], U8, name=f"hs{o}_{u}", align_bytes=64) for u in range(2)] for o in range(PASSES)]
        neg_amax = keep.tile([P, TILES], F32, name="neg_amax")
        lift = keep.tile([P, TILES], F32, name="lift")
        shift = keep.tile([P, TILES], F32, name="shift")
        total = keep.tile([P, TILES], F32, name="total")
        rinv = keep.tile([P, TILES], F32, name="rinv")

        nc.vector.memset(neg_half[:], -0.5)
        nc.gpsimd.memset(xs[:].bitcast(I32), 0)
        for i in range(TILES):
            nc.scalar.activation(ea[i][:, 0:PAD], neg_half[:], ACT.Exp, scale=4096.0)
        make_identity(nc, ident[:])

        for i in range(TILES):
            nc.sync.dma_start(al[i][:], alpha[i * P : (i + 1) * P, :])
        for n, m in enumerate((m1, m2)):
            nc.scalar.dma_start(mcol[n][:], m[0].rearrange("(p b) -> p b", b=BLOCKS))

        def load_h(o, u):
            nc.sync.dma_start(hraw[o][u][:], hT[512 * o : 512 * (o + 1), u * 256 : (u + 1) * 256].rearrange("(p j) v -> p j v", j=4))

        early = [(0, 0), (1, 0), (0, 1)]
        for o, u in early:
            load_h(o, u)
        for q in range(4):
            nc.sync.dma_start(xs[32 * q : 32 * q + 8, :].bitcast(I32), x_scales.bitcast(I32)[:, 4 * q : 4 * q + 4, :])
        nc.sync.dma_start(offs_t[:], offs)
        for o in range(PASSES):
            nc.sync.dma_start(xw[o][:], x_words[o].rearrange("p n t -> p (n t)").bitcast(I32))
        load_h(1, 1)
        nc.sync.dma_start(lab_t[:], lab)

        for i in range(TILES):
            nc.vector.tensor_reduce(neg_amax[:, i : i + 1], al[i][:], AX.X, ALU.max, negate=True)
            nc.scalar.activation(ea[i][:, PAD : PAD + R], al[i][:], ACT.Exp, bias=neg_amax[:, i : i + 1], scale=1.0)
        nc.gpsimd.tensor_scalar(shift[:], neg_amax[:], -0.5, 2.0, ALU.mult, ALU.add)
        nc.gpsimd.tensor_scalar(euler[:], neg_half[:], 0.0, math.e, ALU.mult, ALU.add)
        nc.gpsimd.tensor_tensor(lift[:], euler[:], shift[:], ALU.pow)

        mask = [psum.tile([P, R], F32, name=f"mask{n}", tag=f"root{2 + n}") for n in range(2)]
        for n in range(2):
            for b in range(BLOCKS):
                nc.tensor.transpose(mask[n][:, b * P : (b + 1) * P], mcol[n][:, b : b + 1].to_broadcast([P, P]), ident[:])
        root = []

        def interleave(engine_copy, o, u):
            hb[o, u] = keep.tile([P, V // 2, 4], BF16, name=f"hb{o}_{u}", tag=f"slot{TILES - 1 - 2 * u - o}", align_bytes=64)
            engine_copy(
                hb[o, u][:].rearrange("p (c i) j -> p c j i", i=4),
                hraw[o][u][:].rearrange("p j (c i) -> p c j i", i=4),
            )

        def quantise(o, u):
            hq[o, u] = keep.tile([P, V // 2], U32, name=f"hq{o}_{u}", tag=f"exp{(1 + o + 2 * u) % TILES}", align_bytes=64)
            nc.vector.quantize_mx(out=hq[o, u][:].bitcast(FP8X4), scales=hs[o][u][:], in_=hb[o, u][:].rearrange("p c j -> p (c j)"))

        for o, u in early:
            interleave(nc.scalar.copy, o, u)

        sumT = [psum.tile([P, R], F32, name=f"sumT{i}", tag=f"work{i}") for i in range(TILES)]

        def add_turned(i, term, first, last):
            for b in range(BLOCKS):
                cols = slice(b * P, (b + 1) * P)
                nc.tensor.matmul(
                    sumT[i][:, cols], term[:, cols], ident[:],
                    start=(first and b == 0), stop=(last and b == BLOCKS - 1), is_transpose=True,
                )

        for i in range(TILES):
            add_turned(i, ea[i][:, PAD : PAD + R], True, False)
        for i in range(TILES):
            for n in range(2):
                term = win[i][:, (2 + n) * S : (3 + n) * S]
                nc.vector.tensor_tensor(
                    term.rearrange("p (c b) -> p c b", b=BLOCKS),
                    ea[i][:, PAD - 1 - n : PAD - 1 - n + R].rearrange("p (c b) -> p c b", b=BLOCKS),
                    mask[n][:].rearrange("p (b c) -> p c b", b=BLOCKS),
                    ALU.mult,
                )
                add_turned(i, term, False, n == 1)
            nc.scalar.activation(rootT[i], sumT[i][:], ACT.Sqrt)
        for i in range(TILES):
            root.append(psum.tile([P, R], F32, name=f"root{i}", tag=f"root{i}"))
            for b in range(BLOCKS):
                nc.tensor.transpose(root[i][:, b * P : (b + 1) * P], rootT[i][:, b * P : (b + 1) * P], ident[:])

        for o, u in early:
            quantise(o, u)
        xg = [keep.tile([P, S], U32, name=f"xg{o}", tag=("planes", "words0")[o], align_bytes=64) for o in range(PASSES)]
        sg = keep.tile([P, S], U8, name="sg", tag="slot1", align_bytes=64)
        nc.vector.tensor_copy(sg[:], xs[:].indirect(offs_t[:]))
        nc.vector.tensor_copy(xg[0][:], xw[0][:].bitcast(U32).indirect(offs_t[:]))
        nc.vector.tensor_copy(xg[1][:], xw[1][:].bitcast(U32).indirect(offs_t[:]))

        y = [psum.tile([P, S], F32, name=f"y{i}", tag=f"work{TILES - 1 - i}") for i in range(TILES)]

        def product(i, o):
            u, w = divmod(i, 2)
            cols = slice(w * P, (w + 1) * P)
            nc.tensor.matmul_mx(
                out=y[i][:],
                lhsT=hq[o, u][:, cols].bitcast(FP8X4),
                lhsT_scale=hs[o][u][:, cols],
                rhs=xg[o][:].bitcast(FP8X4),
                rhs_scale=sg[4 * o : P, :],
                start=(o == 0),
                stop=(o == PASSES - 1),
            )

        def row_max_and_sum(i):
            one = slice(i, i + 1)
            nc.vector.tensor_reduce(neg_ymax[:, one], y[i][:], AX.X, ALU.max, negate=True)
            nc.scalar.activation(rootT[TILES - 1 - i], y[i][:], ACT.Exp, bias=neg_ymax[:, one], accum_out=total[:, one])
            nc.gpsimd.tensor_tensor(rinv[:, one], total[:, one], neg_half[:, 0:1], ALU.pow)
            nc.gpsimd.tensor_tensor(scale_t[:, one], rinv[:, one], lift[:, one], ALU.mult)

        def look_up(i):
            nc.vector.tensor_scalar(win[i][:, 0:S], y[i][:], neg_ymax[:, i : i + 1], None, ALU.add)
            nc.scalar.activation(picked[i][:], win[i][:].indirect(lab_t[:]), ACT.Exp, scale=0.5)

        interleave(nc.vector.tensor_copy, 1, 1)
        quantise(1, 1)
        neg_ymax = keep.tile([P, TILES], F32, name="neg_ymax", tag="slot0", align_bytes=64)
        for pair in range(2):
            for o in range(PASSES):
                for i in range(2 * pair, 2 * pair + 2):
                    product(i, o)
        row_max_and_sum(0)
        for i in range(TILES):
            if i + 1 < TILES:
                row_max_and_sum(i + 1)
            look_up(i)
        for i in range(TILES):
            one = slice(i, i + 1)
            pieces = 2 if i == TILES - 1 else 1
            for h in range(pieces):
                cols = slice(h * R // pieces, (h + 1) * R // pieces)
                nc.vector.scalar_tensor_tensor(res[i][:, cols], picked[i][:, cols], scale_t[:, one], root[i][:, cols], ALU.mult, ALU.mult)
                queue = nc.scalar if h == 1 else nc.sync
                queue.dma_start(out[i * P : (i + 1) * P, cols], res[i][:, cols])
